import numpy as np
import ml_dtypes


def mxq(x, axis, fmt="e4m3"):
    dtype, down = {"e4m3": (ml_dtypes.float8_e4m3fn, 7), "e5m2": (ml_dtypes.float8_e5m2, 14)}[fmt]
    v = np.moveaxis(np.asarray(x, np.float32).astype(ml_dtypes.bfloat16).astype(np.float64), axis, -1)
    blocks = v.reshape(v.shape[:-1] + (-1, 32))
    amax = np.abs(blocks).max(-1, keepdims=True)
    byte = np.maximum(np.where(amax > 0, np.frexp(amax)[1] - 1 + 127, 0) - down, 1)
    scale = np.exp2(byte - 127.0)
    codes = (blocks / scale).astype(np.float32).astype(dtype).astype(np.float64)
    return np.moveaxis((codes * scale).reshape(v.shape), -1, axis)


WIDE = False


def mx_kscale(k):
    if not WIDE:
        return np.ones(k)
    levels = np.array([10, -10, 5, -5, 0])
    if k % 512:
        return np.exp2(np.random.permutation(np.resize(levels, k // 32))).repeat(32)
    a = np.empty((k // 512, 16))
    for p in range(k // 512):
        a[p, :8] = np.random.permutation(np.resize(levels, 8))
        for g in range(8):
            far = levels[np.abs(levels - a[p, g]) >= 10]
            a[p, g + 8] = far[np.random.randint(len(far))]
    return np.exp2(a.ravel()).repeat(32)


def f64(x):
    return np.asarray(x).astype(np.float64)


def striped(idx):
    return np.tile(idx.reshape(-1, 16).T, (8, 1)).astype(np.uint16)


def unstriped(offs):
    return offs[:16].T.reshape(-1).astype(np.int64)


def striped8(idx):
    return np.concatenate([x.reshape(-1, 16).T for x in idx]).astype(np.uint16)


def runs(offs, k):
    lists = np.stack([offs[16 * r : 16 * r + 16].T.reshape(-1) for r in range(8)]).astype(np.int64)
    return lists[np.arange(k) % 512 // 64]


def pack_weight(w):
    k, n = w.shape
    w = f64(np.asarray(w, np.float32).astype(ml_dtypes.bfloat16)).reshape(k // 32, 32, n)
    amax = np.abs(w).max(1)
    byte = np.clip(np.where(amax > 0, np.frexp(amax)[1] - 1 + 127 - 7, 1), 1, 254)
    scaled = (w * np.exp2(127.0 - byte)[:, None, :]).reshape(k, n).astype(np.float32)
    words = np.ascontiguousarray(scaled.reshape(k // 512, 128, 4, n).transpose(0, 1, 3, 2)).astype(ml_dtypes.float8_e4m3fn).view(np.uint8)
    return words, np.ascontiguousarray(byte.astype(np.uint8).reshape(k // 512, 16, n))


def unpack_weight(words, scales):
    g, p, n, _ = words.shape
    vals = np.ascontiguousarray(words).view(ml_dtypes.float8_e4m3fn).astype(np.float64) * np.repeat(np.exp2(scales.astype(np.float64) - 127.0), 8, axis=1)[..., None]
    return vals.transpose(0, 1, 3, 2).reshape(g * 512, n)


def sigmoid(v):
    return 1.0 / (1.0 + np.exp(-np.maximum(v, -700.0)))


K, T, S, H, W, C = 512, 2048, 512, 512, 256, 512


def setup_inputs():
    n = np.random.standard_normal
    s = mx_kscale(K)[:, None]
    packed_xT = pack_weight(n((K, T)) * s)
    perm = np.stack([np.random.permutation(S) for _ in range(8)])
    return {
        "x_words": packed_xT[0],
        "x_scales": packed_xT[1],
        "w1": (n((K, H)) / np.sqrt(K) / s).astype(np.float32),
        "gs": (np.random.uniform(0.5, 1.5, (K, 1)) / s).astype(np.float32),
        "offs": striped(np.random.permutation(T)[:S]),
        "n1": striped8(perm[:, :W]),
        "n2": striped8(perm[:, W:]),
        "cand": striped(np.random.permutation(T)[:C]),
        "n3": striped8(np.stack([np.random.permutation(S) for _ in range(8)])),
    }


def reference(x_words, x_scales, w1, gs, offs, n1, n2, cand, n3):
    x_cand = unpack_weight(x_words, x_scales)[:, unstriped(cand)]
    xq = unpack_weight(x_words, x_scales)[:, unstriped(offs)]
    y = mxq(f64(w1), 0, "e4m3").T @ xq
    pb = y[np.arange(H)[:, None], runs(n2, H)]
    pa = y[np.arange(H)[:, None], runs(n1, H)]
    rb = pb * sigmoid(pb - pa)
    ra = pa * sigmoid(pa - pb)
    ds = np.zeros((H, S))
    ds[np.arange(H)[:, None], runs(n1, H)] = ra
    dt = ds.copy()
    dt[np.arange(H)[:, None], runs(n2, H)] = rb
    z = f64(gs) * dt
    s = 0.0625 * ((x_cand.T @ mxq(z, 0, "e4m3")))
    return s - (s[np.arange(C)[:, None], runs(n3, C)])

@@ -1,0 +1,161 @@
+from contextlib import ExitStack
+
+import concourse.mybir as mybir
+
+F32 = mybir.dt.float32
+BF16 = mybir.dt.bfloat16
+I32 = mybir.dt.int32
+U32 = mybir.dt.uint32
+U16 = mybir.dt.uint16
+U8 = mybir.dt.uint8
+FP8X4 = mybir.dt.float8_e4m3fn_x4
+ACT = mybir.ActivationFunctionType
+ALU = mybir.AluOpType
+
+P = 128
+PACK = 4
+K, T, S, H, W, C = 512, 2048, 512, 512, 256, 512
+HALF = S // 2
+W_PIECES = ((0, 256), (256, 384), (384, 512))
+TILE_ORDER = (2, 0, 1, 3)
+FLOPS = 2 * K * H * S + 2 * H * C * S
+
+
+def tile_picked_canddueldif_none_p_kernel(tc, x_words, x_scales, w1, gs, offs, n1, n2, cand, n3, out):
+    nc = tc.nc
+    with ExitStack() as ctx:
+        keep = ctx.enter_context(tc.tile_pool(name="keep", bufs=1))
+        psum = ctx.enter_context(tc.psum_pool(name="psum", bufs=1))
+
+        def load_list(src, name):
+            tile = keep.tile(list(src.shape), U16, name=name)
+            nc.sync.dma_start(tile[:], src)
+            return tile
+
+        x_sc = keep.tile([P, T], U8, align_bytes=64)
+        nc.vector.memset(x_sc[:].bitcast(I32), 0)
+
+        offs_t = load_list(offs, "offs_t")
+        cand_t = load_list(cand, "cand_t")
+        for q in range(4):
+            nc.sync.dma_start(x_sc[32 * q : 32 * q + 4, :].bitcast(I32), x_scales[0, 4 * q : 4 * q + 4, :].bitcast(I32))
+        n1_t = load_list(n1, "n1_t")
+        x_w = keep.tile([P, T], U32, align_bytes=64)
+        nc.sync.dma_start(x_w[:].bitcast(I32), x_words[0].rearrange("p n t -> p (n t)").bitcast(I32))
+        w_rows = w1.rearrange("(p j) c -> p j c", j=PACK)
+        w_raw = []
+        for u, (c0, c1) in enumerate(W_PIECES):
+            piece = keep.tile([P, PACK, c1 - c0], F32, name="w_raw%d" % u)
+            nc.sync.dma_start(piece[:], w_rows[:, :, c0:c1])
+            w_raw.append(piece)
+
+        n2_t = load_list(n2, "n2_t")
+        gain = keep.tile([P, PACK], F32)
+        nc.sync.dma_start(gain[:], gs.rearrange("(p t) o -> p (t o)", t=PACK))
+        n3_t = load_list(n3, "n3_t")
+
+        warm = keep.tile([P, 1], F32)
+        warm_out = keep.tile([P, 1], F32)
+        nc.vector.memset(warm[:], 0.0)
+        nc.scalar.activation(warm_out[:], warm[:], ACT.Sigmoid)
+
+        xq_sc = keep.tile([P, S], U8, align_bytes=64)
+        nc.vector.tensor_copy(xq_sc[:], x_sc[:].indirect(offs_t[:]))
+        xq_w = keep.tile([P, S], U32, align_bytes=64)
+        nc.vector.tensor_copy(xq_w[:], x_w[:].indirect(offs_t[:]))
+
+        w_bf = keep.tile([P, H * PACK], BF16, align_bytes=64)
+        w_bf_v = w_bf[:].rearrange("p (t m j) -> p m j t", t=PACK, j=PACK)
+        for u, (c0, c1) in enumerate(W_PIECES):
+            dst = w_bf_v[:, c0 // PACK : c1 // PACK, :, :]
+            src = w_raw[u][:].rearrange("p j (m t) -> p m j t", t=PACK)
+            if u == 0:
+                nc.scalar.copy(dst, src)
+            else:
+                nc.vector.tensor_copy(dst, src)
+        w_q = keep.tile([P, H], U32, align_bytes=64)
+        w_sc = keep.tile([P, H], U8, align_bytes=64)
+        for c0, c1 in ((256, 384), (0, 256), (384, 512)):
+            nc.vector.quantize_mx(w_q[:, c0:c1].bitcast(FP8X4), w_sc[:, c0:c1], w_bf[:, PACK * c0 : PACK * c1])
+
+        xc_sc_list = keep.tile([P, C], U8, align_bytes=64)
+        nc.vector.tensor_copy(xc_sc_list[:], x_sc[:].indirect(cand_t[:]))
+        xc_w = keep.tile([P, C], U32, align_bytes=64)
+        nc.vector.tensor_copy(xc_w[:].rearrange("p (t m) -> p m t", t=PACK), x_w[:].indirect(cand_t[:]))
+        xc_sc = keep.tile([P, C], U8, align_bytes=64)
+        nc.vector.tensor_copy(xc_sc[:].rearrange("p (t m) -> p m t", t=PACK), xc_sc_list[:].rearrange("p (m t) -> p m t", t=PACK))
+
+        y = {}
+        for t in TILE_ORDER:
+            cols = slice(P * t, P * (t + 1))
+            acc = psum.tile([P, S], F32, name="y_acc%d" % t, tag="bank%d" % (4 + t))
+            nc.tensor.matmul_mx(acc[:], w_q[:, cols].bitcast(FP8X4), w_sc[:, cols], xq_w[:].bitcast(FP8X4), xq_sc[:], start=True, stop=True)
+            y[t] = keep.tile([P, S], F32, name="y%d" % t)
+            nc.scalar.copy(y[t][:], acc[:])
+
+
+        z_bf = keep.tile([P, S, PACK], BF16, align_bytes=64)
+        pa = keep.tile([P, PACK, W], F32)
+        pb = keep.tile([P, PACK, W], F32)
+        diff = keep.tile([P, PACK, W], F32)
+        sa = keep.tile([P, PACK, W], F32)
+        sb = keep.tile([P, PACK, W], F32)
+        dt = [keep.tile([P, S], F32, name="dt%d" % t) for t in range(PACK)]
+
+        def duel(a, b):
+            nc.vector.tensor_tensor(diff[:, a:b, :], pa[:, a:b, :], pb[:, a:b, :], ALU.subtract)
+            for i in range(a, b):
+                nc.scalar.activation(sa[:, i, :], diff[:, i, :], ACT.Sigmoid)
+                nc.scalar.activation(sb[:, i, :], diff[:, i, :], ACT.Sigmoid, scale=-1.0)
+
+        def put_a(i):
+            nc.vector.tensor_tensor(dt[TILE_ORDER[i]][:].indirect(n1_t[:]), pa[:, i, :], sa[:, i, :], ALU.mult)
+
+        def put_b(i):
+            t = TILE_ORDER[i]
+            nc.vector.tensor_tensor(dt[t][:].indirect(n2_t[:]), pb[:, i, :], sb[:, i, :], ALU.mult)
+            if t == 2:
+                nc.scalar.activation(z_bf[:, :, 2:4], dt[t][:].unsqueeze(2).to_broadcast([P, S, 2]), ACT.Copy, scale=gain[:, t : t + 1])
+            elif t < 2:
+                nc.scalar.activation(z_bf[:, :, t], dt[t][:], ACT.Copy, scale=gain[:, t : t + 1])
+
+        for i, t in enumerate(TILE_ORDER):
+            nc.vector.tensor_copy(pa[:, i, :], y[t][:].indirect(n1_t[:]))
+            if i == 2:
+                duel(0, 2)
+            nc.vector.tensor_copy(pb[:, i, :], y[t][:].indirect(n2_t[:]))
+        put_a(0)
+        duel(2, 4)
+        for i in range(PACK):
+            if i + 1 < PACK:
+                put_a(i + 1)
+            put_b(i)
+
+
+        z_q = keep.tile([P, S], U32, align_bytes=64)
+        z_sc = keep.tile([P, S], U8, align_bytes=64)
+        halves = [slice(u * HALF, (u + 1) * HALF) for u in range(2)]
+        for part in halves:
+            nc.vector.tensor_scalar(z_bf[:, part, 3], dt[3][:, part], gain[:, 3:4], None, ALU.mult)
+        for part in halves:
+            nc.vector.quantize_mx(z_q[:, part].bitcast(FP8X4), z_sc[:, part], z_bf[:, part, :].rearrange("p s t -> p (s t)"))
+
+        out_rows = out.rearrange("(p t) s -> p t s", t=PACK)
+        for t in range(PACK):
+            cols = slice(P * t, P * (t + 1))
+            neg = keep.tile([P, S], F32, name="neg%d" % t)
+            acc = []
+            for u, part in enumerate(halves):
+                bank = psum.tile([P, HALF], F32, name="s_acc%d_%d" % (t, u), tag="bank%d" % (2 * t + u))
+                nc.tensor.matmul_mx(bank[:], xc_w[:, cols].bitcast(FP8X4), xc_sc[:, cols], z_q[:, part].bitcast(FP8X4), z_sc[:, part], start=True, stop=True)
+                nc.scalar.activation(neg[:, part], bank[:], ACT.Copy, scale=-0.0625)
+                acc.append(bank)
+            for u, part in enumerate(halves):
+                pos = keep.tile([P, HALF], F32, name="pos%d_%d" % (t, u))
+                if t == 0 and u == 0:
+                    nc.vector.tensor_scalar(pos[:], acc[u][:], 0.0625, None, ALU.mult)
+                else:
+                    nc.scalar.activation(pos[:], acc[u][:], ACT.Copy, scale=0.0625)
+                res = keep.tile([P, HALF], F32, name="res%d_%d" % (t, u))
+                nc.vector.tensor_tensor(res[:], neg[:].indirect(n3_t[:, 16 * u : 16 * (u + 1)]), pos[:], ALU.add)
+                nc.sync.dma_start(out_rows[:, t, part], res[:])

@@ -16,7 +16,7 @@ P = 128
 PACK = 4
 K, T, S, H, W, C = 512, 2048, 512, 512, 256, 512
 HALF = S // 2
-W_PIECES = ((0, 256), (256, 384), (384, 512))
+M_SCALAR = 64
 TILE_ORDER = (2, 0, 1, 3)
 FLOPS = 2 * K * H * S + 2 * H * C * S
 
@@ -39,16 +39,12 @@ def tile_picked_canddueldif_none_p_kernel(tc, x_words, x_scales, w1, gs, offs, n
         cand_t = load_list(cand, "cand_t")
         for q in range(4):
             nc.sync.dma_start(x_sc[32 * q : 32 * q + 4, :].bitcast(I32), x_scales[0, 4 * q : 4 * q + 4, :].bitcast(I32))
-        n1_t = load_list(n1, "n1_t")
+
+        w_raw = keep.tile([P, PACK, H], F32)
+        nc.sync.dma_start(w_raw[:], w1.rearrange("(p j) c -> p j c", j=PACK))
         x_w = keep.tile([P, T], U32, align_bytes=64)
         nc.sync.dma_start(x_w[:].bitcast(I32), x_words[0].rearrange("p n t -> p (n t)").bitcast(I32))
-        w_rows = w1.rearrange("(p j) c -> p j c", j=PACK)
-        w_raw = []
-        for u, (c0, c1) in enumerate(W_PIECES):
-            piece = keep.tile([P, PACK, c1 - c0], F32, name="w_raw%d" % u)
-            nc.sync.dma_start(piece[:], w_rows[:, :, c0:c1])
-            w_raw.append(piece)
-
+        n1_t = load_list(n1, "n1_t")
         n2_t = load_list(n2, "n2_t")
         gain = keep.tile([P, PACK], F32)
         nc.sync.dma_start(gain[:], gs.rearrange("(p t) o -> p (t o)", t=PACK))
@@ -61,37 +57,35 @@ def tile_picked_canddueldif_none_p_kernel(tc, x_words, x_scales, w1, gs, offs, n
 
         xq_sc = keep.tile([P, S], U8, align_bytes=64)
         nc.vector.tensor_copy(xq_sc[:], x_sc[:].indirect(offs_t[:]))
-        xq_w = keep.tile([P, S], U32, align_bytes=64)
-        nc.vector.tensor_copy(xq_w[:], x_w[:].indirect(offs_t[:]))
+        xc_sc_list = keep.tile([P, C], U8, align_bytes=64)
+        nc.vector.tensor_copy(xc_sc_list[:], x_sc[:].indirect(cand_t[:]))
 
         w_bf = keep.tile([P, H * PACK], BF16, align_bytes=64)
         w_bf_v = w_bf[:].rearrange("p (t m j) -> p m j t", t=PACK, j=PACK)
-        for u, (c0, c1) in enumerate(W_PIECES):
-            dst = w_bf_v[:, c0 // PACK : c1 // PACK, :, :]
-            src = w_raw[u][:].rearrange("p j (m t) -> p m j t", t=PACK)
-            if u == 0:
-                nc.scalar.copy(dst, src)
-            else:
-                nc.vector.tensor_copy(dst, src)
-        w_q = keep.tile([P, H], U32, align_bytes=64)
-        w_sc = keep.tile([P, H], U8, align_bytes=64)
-        for c0, c1 in ((256, 384), (0, 256), (384, 512)):
-            nc.vector.quantize_mx(w_q[:, c0:c1].bitcast(FP8X4), w_sc[:, c0:c1], w_bf[:, PACK * c0 : PACK * c1])
-
-        xc_sc_list = keep.tile([P, C], U8, align_bytes=64)
-        nc.vector.tensor_copy(xc_sc_list[:], x_sc[:].indirect(cand_t[:]))
-        xc_w = keep.tile([P, C], U32, align_bytes=64)
-        nc.vector.tensor_copy(xc_w[:].rearrange("p (t m) -> p m t", t=PACK), x_w[:].indirect(cand_t[:]))
+        w_raw_v = w_raw[:].rearrange("p j (m t) -> p m j t", t=PACK)
+        nc.scalar.copy(w_bf_v[:, :M_SCALAR, :, :], w_raw_v[:, :M_SCALAR, :, :])
+        nc.vector.tensor_copy(w_bf_v[:, M_SCALAR:, :, :], w_raw_v[:, M_SCALAR:, :, :])
         xc_sc = keep.tile([P, C], U8, align_bytes=64)
         nc.vector.tensor_copy(xc_sc[:].rearrange("p (t m) -> p m t", t=PACK), xc_sc_list[:].rearrange("p (m t) -> p m t", t=PACK))
+        w_q = keep.tile([P, H], U32, align_bytes=64)
+        w_sc = keep.tile([P, H], U8, align_bytes=64)
+        nc.vector.quantize_mx(w_q[:].bitcast(FP8X4), w_sc[:], w_bf[:])
 
+        xq_w = keep.tile([P, S], U32, align_bytes=64)
+        for u in range(2):
+            nc.vector.tensor_copy(xq_w[:, u * HALF : (u + 1) * HALF], x_w[:].indirect(offs_t[:, 16 * u : 16 * (u + 1)]))
+        xc_w = keep.tile([P, C], U32, align_bytes=64)
+        nc.vector.tensor_copy(xc_w[:].rearrange("p (t m) -> p m t", t=PACK), x_w[:].indirect(cand_t[:]))
+
+        halves = [slice(u * HALF, (u + 1) * HALF) for u in range(2)]
         y = {}
-        for t in TILE_ORDER:
+        for i, t in enumerate(TILE_ORDER):
             cols = slice(P * t, P * (t + 1))
-            acc = psum.tile([P, S], F32, name="y_acc%d" % t, tag="bank%d" % (4 + t))
-            nc.tensor.matmul_mx(acc[:], w_q[:, cols].bitcast(FP8X4), w_sc[:, cols], xq_w[:].bitcast(FP8X4), xq_sc[:], start=True, stop=True)
             y[t] = keep.tile([P, S], F32, name="y%d" % t)
-            nc.scalar.copy(y[t][:], acc[:])
+            for u, part in enumerate(halves if i == 0 else [slice(0, S)]):
+                acc = psum.tile([P, part.stop - part.start], F32, name="y_acc%d_%d" % (t, u), tag="bank%d" % (7 if u else 3 + i))
+                nc.tensor.matmul_mx(acc[:], w_q[:, cols].bitcast(FP8X4), w_sc[:, cols], xq_w[:, part].bitcast(FP8X4), xq_sc[:, part], start=True, stop=True)
+                nc.scalar.copy(y[t][:, part], acc[:])
 
 
         z_bf = keep.tile([P, S, PACK], BF16, align_bytes=64)
@@ -134,7 +128,6 @@ def tile_picked_canddueldif_none_p_kernel(tc, x_words, x_scales, w1, gs, offs, n
 
         z_q = keep.tile([P, S], U32, align_bytes=64)
         z_sc = keep.tile([P, S], U8, align_bytes=64)
-        halves = [slice(u * HALF, (u + 1) * HALF) for u in range(2)]
         for part in halves:
             nc.vector.tensor_scalar(z_bf[:, part, 3], dt[3][:, part], gain[:, 3:4], None, ALU.mult)
         for part in halves:
@@ -145,17 +138,17 @@ def tile_picked_canddueldif_none_p_kernel(tc, x_words, x_scales, w1, gs, offs, n
             cols = slice(P * t, P * (t + 1))
             neg = keep.tile([P, S], F32, name="neg%d" % t)
             acc = []
-            for u, part in enumerate(halves):
-                bank = psum.tile([P, HALF], F32, name="s_acc%d_%d" % (t, u), tag="bank%d" % (2 * t + u))
+            for u, part in enumerate(halves if t == 0 else [slice(0, S)]):
+                bank = psum.tile([P, part.stop - part.start], F32, name="s_acc%d_%d" % (t, u), tag="bank%d" % (t + 1 if t else u))
                 nc.tensor.matmul_mx(bank[:], xc_w[:, cols].bitcast(FP8X4), xc_sc[:, cols], z_q[:, part].bitcast(FP8X4), z_sc[:, part], start=True, stop=True)
                 nc.scalar.activation(neg[:, part], bank[:], ACT.Copy, scale=-0.0625)
-                acc.append(bank)
+                acc.extend([bank[:]] if t == 0 else [bank[:, h] for h in halves])
             for u, part in enumerate(halves):
                 pos = keep.tile([P, HALF], F32, name="pos%d_%d" % (t, u))
                 if t == 0 and u == 0:
-                    nc.vector.tensor_scalar(pos[:], acc[u][:], 0.0625, None, ALU.mult)
+                    nc.vector.tensor_scalar(pos[:], acc[u], 0.0625, None, ALU.mult)
                 else:
-                    nc.scalar.activation(pos[:], acc[u][:], ACT.Copy, scale=0.0625)
+                    nc.scalar.activation(pos[:], acc[u], ACT.Copy, scale=0.0625)
                 res = keep.tile([P, HALF], F32, name="res%d_%d" % (t, u))
                 nc.vector.tensor_tensor(res[:], neg[:].indirect(n3_t[:, 16 * u : 16 * (u + 1)]), pos[:], ALU.add)
                 nc.sync.dma_start(out_rows[:, t, part], res[:])

@@ -96,8 +96,8 @@ def tile_picked_canddueldif_none_p_kernel(tc, x_words, x_scales, w1, gs, offs, n
         sb = keep.tile([P, PACK, W], F32)
         dt = [keep.tile([P, S], F32, name="dt%d" % t) for t in range(PACK)]
 
-        def duel(a, b):
-            nc.vector.tensor_tensor(diff[:, a:b, :], pa[:, a:b, :], pb[:, a:b, :], ALU.subtract)
+        def duel(a, b, engine):
+            engine.tensor_tensor(diff[:, a:b, :], pa[:, a:b, :], pb[:, a:b, :], ALU.subtract)
             for i in range(a, b):
                 nc.scalar.activation(sa[:, i, :], diff[:, i, :], ACT.Sigmoid)
                 nc.scalar.activation(sb[:, i, :], diff[:, i, :], ACT.Sigmoid, scale=-1.0)
@@ -115,11 +115,11 @@ def tile_picked_canddueldif_none_p_kernel(tc, x_words, x_scales, w1, gs, offs, n
 
         for i, t in enumerate(TILE_ORDER):
             nc.vector.tensor_copy(pa[:, i, :], y[t][:].indirect(n1_t[:]))
-            if i == 2:
-                duel(0, 2)
             nc.vector.tensor_copy(pb[:, i, :], y[t][:].indirect(n2_t[:]))
+            if i < 3:
+                duel(i, i + 1, nc.gpsimd)
         put_a(0)
-        duel(2, 4)
+        duel(3, 4, nc.vector)
         for i in range(PACK):
             if i + 1 < PACK:
                 put_a(i + 1)

@@ -1,6 +1,7 @@
 from contextlib import ExitStack
 
 import concourse.mybir as mybir
+from concourse.masks import make_identity
 
 F32 = mybir.dt.float32
 BF16 = mybir.dt.bfloat16
@@ -38,7 +39,7 @@ def tile_picked_canddueldif_none_p_kernel(tc, x_words, x_scales, w1, gs, offs, n
         offs_t = load_list(offs, "offs_t")
         cand_t = load_list(cand, "cand_t")
         for q in range(4):
-            nc.sync.dma_start(x_sc[32 * q : 32 * q + 4, :].bitcast(I32), x_scales[0, 4 * q : 4 * q + 4, :].bitcast(I32))
+            (nc.sync if q < 2 else nc.scalar).dma_start(x_sc[32 * q : 32 * q + 4, :].bitcast(I32), x_scales[0, 4 * q : 4 * q + 4, :].bitcast(I32))
 
         w_raw = keep.tile([P, PACK, H], F32)
         nc.sync.dma_start(w_raw[:], w1.rearrange("(p j) c -> p j c", j=PACK))
@@ -88,26 +89,48 @@ def tile_picked_canddueldif_none_p_kernel(tc, x_words, x_scales, w1, gs, offs, n
                 nc.scalar.copy(y[t][:, part], acc[:])
 
 
-        z_bf = keep.tile([P, S, PACK], BF16, align_bytes=64)
         pa = keep.tile([P, PACK, W], F32)
         pb = keep.tile([P, PACK, W], F32)
-        diff = keep.tile([P, PACK, W], F32)
+        diff = keep.tile([P, W], F32)
         sa = keep.tile([P, PACK, W], F32)
-        sb = keep.tile([P, PACK, W], F32)
         dt = [keep.tile([P, S], F32, name="dt%d" % t) for t in range(PACK)]
 
-        def duel(a, b, engine):
-            engine.tensor_tensor(diff[:, a:b, :], pa[:, a:b, :], pb[:, a:b, :], ALU.subtract)
-            for i in range(a, b):
-                nc.scalar.activation(sa[:, i, :], diff[:, i, :], ACT.Sigmoid)
-                nc.scalar.activation(sb[:, i, :], diff[:, i, :], ACT.Sigmoid, scale=-1.0)
+        ident = keep.tile([P, P], F32)
+        make_identity(nc, ident[:])
+        turned_a = keep.tile([P, PACK, W], F32, tag="stage", align_bytes=64)
+        turned_b = keep.tile([P, PACK, W], F32)
+        sb = [turned_b[:, (i + 1) % PACK, :] for i in range(PACK)]
+        d = {}
+        blocks = [slice(b * P, (b + 1) * P) for b in range(W // P)]
+
+        def duel(i):
+            if i == 0:
+                nc.vector.tensor_tensor(diff[:], pa[:, i, :], pb[:, i, :], ALU.subtract)
+                d[i] = diff[:]
+            else:
+                there = psum.tile([P, 2, W], F32, name="there%d" % i, tag="bank%d" % (0, 1, 2)[i - 1])
+                for s, src in enumerate((pa, pb)):
+                    for b in blocks:
+                        nc.tensor.transpose(there[:, s, b], src[:, i, b], ident[:])
+                nc.scalar.copy(turned_a[:, i, :], there[:, 0, :])
+                nc.scalar.activation(turned_b[:, i, :], there[:, 1, :], ACT.Copy, scale=-1.0)
+                back = psum.tile([P, W], F32, name="back%d" % i, tag="bank%d" % (2, 7, 3)[i - 1])
+                for b in blocks:
+                    for s, src in enumerate((turned_a, turned_b)):
+                        nc.tensor.matmul(back[:, b], src[:, i, b], ident[:], start=(s == 0), stop=(s == 1), is_transpose=True)
+                d[i] = back[:]
+            nc.scalar.activation(sa[:, i, :], d[i], ACT.Sigmoid)
+            if i > 0:
+                nc.scalar.activation(sb[i - 1], d[i - 1], ACT.Sigmoid, scale=-1.0)
+            if i == PACK - 1:
+                nc.scalar.activation(sb[i], d[i], ACT.Sigmoid, scale=-1.0)
 
         def put_a(i):
             nc.vector.tensor_tensor(dt[TILE_ORDER[i]][:].indirect(n1_t[:]), pa[:, i, :], sa[:, i, :], ALU.mult)
 
         def put_b(i):
             t = TILE_ORDER[i]
-            nc.vector.tensor_tensor(dt[t][:].indirect(n2_t[:]), pb[:, i, :], sb[:, i, :], ALU.mult)
+            nc.vector.tensor_tensor(dt[t][:].indirect(n2_t[:]), pb[:, i, :], sb[i], ALU.mult)
             if t == 2:
                 nc.scalar.activation(z_bf[:, :, 2:4], dt[t][:].unsqueeze(2).to_broadcast([P, S, 2]), ACT.Copy, scale=gain[:, t : t + 1])
             elif t < 2:
@@ -115,11 +138,13 @@ def tile_picked_canddueldif_none_p_kernel(tc, x_words, x_scales, w1, gs, offs, n
 
         for i, t in enumerate(TILE_ORDER):
             nc.vector.tensor_copy(pa[:, i, :], y[t][:].indirect(n1_t[:]))
+            if i == 1:
+                duel(0)
             nc.vector.tensor_copy(pb[:, i, :], y[t][:].indirect(n2_t[:]))
-            if i < 3:
-                duel(i, i + 1, nc.gpsimd)
+            if i > 0:
+                duel(i)
+        z_bf = keep.tile([P, S, PACK], BF16, tag="stage", align_bytes=64)
         put_a(0)
-        duel(3, 4, nc.vector)
         for i in range(PACK):
             if i + 1 < PACK:
                 put_a(i + 1)

@@ -18,7 +18,7 @@ PACK = 4
 K, T, S, H, W, C = 512, 2048, 512, 512, 256, 512
 HALF = S // 2
 M_SCALAR = 64
-TILE_ORDER = (2, 0, 1, 3)
+TILE_ORDER = (0, 2, 1, 3)
 FLOPS = 2 * K * H * S + 2 * H * C * S
 
 
@@ -39,7 +39,7 @@ def tile_picked_canddueldif_none_p_kernel(tc, x_words, x_scales, w1, gs, offs, n
         offs_t = load_list(offs, "offs_t")
         cand_t = load_list(cand, "cand_t")
         for q in range(4):
-            (nc.sync if q < 2 else nc.scalar).dma_start(x_sc[32 * q : 32 * q + 4, :].bitcast(I32), x_scales[0, 4 * q : 4 * q + 4, :].bitcast(I32))
+            nc.sync.dma_start(x_sc[32 * q : 32 * q + 4, :].bitcast(I32), x_scales[0, 4 * q : 4 * q + 4, :].bitcast(I32))
 
         w_raw = keep.tile([P, PACK, H], F32)
         nc.sync.dma_start(w_raw[:], w1.rearrange("(p j) c -> p j c", j=PACK))
@@ -51,6 +51,9 @@ def tile_picked_canddueldif_none_p_kernel(tc, x_words, x_scales, w1, gs, offs, n
         nc.sync.dma_start(gain[:], gs.rearrange("(p t) o -> p (t o)", t=PACK))
         n3_t = load_list(n3, "n3_t")
 
+        ident = keep.tile([P, P], F32)
+        nc.vector.memset(ident[:], 0.0)
+        make_identity(nc, ident[:], nomemset=True)
         warm = keep.tile([P, 1], F32)
         warm_out = keep.tile([P, 1], F32)
         nc.vector.memset(warm[:], 0.0)
@@ -95,8 +98,6 @@ def tile_picked_canddueldif_none_p_kernel(tc, x_words, x_scales, w1, gs, offs, n
         sa = keep.tile([P, PACK, W], F32)
         dt = [keep.tile([P, S], F32, name="dt%d" % t) for t in range(PACK)]
 
-        ident = keep.tile([P, P], F32)
-        make_identity(nc, ident[:])
         turned_a = keep.tile([P, PACK, W], F32, tag="stage", align_bytes=64)
         turned_b = keep.tile([P, PACK, W], F32)
         sb = [turned_b[:, (i + 1) % PACK, :] for i in range(PACK)]
@@ -108,7 +109,7 @@ def tile_picked_canddueldif_none_p_kernel(tc, x_words, x_scales, w1, gs, offs, n
                 nc.vector.tensor_tensor(diff[:], pa[:, i, :], pb[:, i, :], ALU.subtract)
                 d[i] = diff[:]
             else:
-                there = psum.tile([P, 2, W], F32, name="there%d" % i, tag="bank%d" % (0, 1, 2)[i - 1])
+                there = psum.tile([P, 2, W], F32, name="there%d" % i, tag="bank0")
                 for s, src in enumerate((pa, pb)):
                     for b in blocks:
                         nc.tensor.transpose(there[:, s, b], src[:, i, b], ident[:])

from contextlib import ExitStack

import concourse.mybir as mybir
from concourse.masks import make_identity

F32 = mybir.dt.float32
BF16 = mybir.dt.bfloat16
I32 = mybir.dt.int32
U32 = mybir.dt.uint32
U16 = mybir.dt.uint16
U8 = mybir.dt.uint8
FP8X4 = mybir.dt.float8_e4m3fn_x4
ACT = mybir.ActivationFunctionType
ALU = mybir.AluOpType

P = 128
PACK = 4
K, T, S, H, W, C = 512, 2048, 512, 512, 256, 512
HALF = S // 2
M_SCALAR = 64
TILE_ORDER = (0, 2, 1, 3)
FLOPS = 2 * K * H * S + 2 * H * C * S


def tile_picked_canddueldif_none_p_kernel(tc, x_words, x_scales, w1, gs, offs, n1, n2, cand, n3, out):
    nc = tc.nc
    with ExitStack() as ctx:
        keep = ctx.enter_context(tc.tile_pool(name="keep", bufs=1))
        psum = ctx.enter_context(tc.psum_pool(name="psum", bufs=1))

        def load_list(src, name):
            tile = keep.tile(list(src.shape), U16, name=name)
            nc.sync.dma_start(tile[:], src)
            return tile

        x_sc = keep.tile([P, T], U8, align_bytes=64)
        nc.vector.memset(x_sc[:].bitcast(I32), 0)

        offs_t = load_list(offs, "offs_t")
        cand_t = load_list(cand, "cand_t")
        for q in range(4):
            nc.sync.dma_start(x_sc[32 * q : 32 * q + 4, :].bitcast(I32), x_scales[0, 4 * q : 4 * q + 4, :].bitcast(I32))

        w_raw = keep.tile([P, PACK, H], F32)
        nc.sync.dma_start(w_raw[:], w1.rearrange("(p j) c -> p j c", j=PACK))
        x_w = keep.tile([P, T], U32, align_bytes=64)
        nc.sync.dma_start(x_w[:].bitcast(I32), x_words[0].rearrange("p n t -> p (n t)").bitcast(I32))
        n1_t = load_list(n1, "n1_t")
        n2_t = load_list(n2, "n2_t")
        gain = keep.tile([P, PACK], F32)
        nc.sync.dma_start(gain[:], gs.rearrange("(p t) o -> p (t o)", t=PACK))
        n3_t = load_list(n3, "n3_t")

        ident = keep.tile([P, P], F32)
        nc.vector.memset(ident[:], 0.0)
        make_identity(nc, ident[:], nomemset=True)
        warm = keep.tile([P, 1], F32)
        warm_out = keep.tile([P, 1], F32)
        nc.vector.memset(warm[:], 0.0)
        nc.scalar.activation(warm_out[:], warm[:], ACT.Sigmoid)

        xq_sc = keep.tile([P, S], U8, align_bytes=64)
        nc.vector.tensor_copy(xq_sc[:], x_sc[:].indirect(offs_t[:]))
        xc_sc_list = keep.tile([P, C], U8, align_bytes=64)
        nc.vector.tensor_copy(xc_sc_list[:], x_sc[:].indirect(cand_t[:]))

        w_bf = keep.tile([P, H * PACK], BF16, align_bytes=64)
        w_bf_v = w_bf[:].rearrange("p (t m j) -> p m j t", t=PACK, j=PACK)
        w_raw_v = w_raw[:].rearrange("p j (m t) -> p m j t", t=PACK)
        nc.scalar.copy(w_bf_v[:, :M_SCALAR, :, :], w_raw_v[:, :M_SCALAR, :, :])
        nc.vector.tensor_copy(w_bf_v[:, M_SCALAR:, :, :], w_raw_v[:, M_SCALAR:, :, :])
        xc_sc = keep.tile([P, C], U8, align_bytes=64)
        nc.vector.tensor_copy(xc_sc[:].rearrange("p (t m) -> p m t", t=PACK), xc_sc_list[:].rearrange("p (m t) -> p m t", t=PACK))
        w_q = keep.tile([P, H], U32, align_bytes=64)
        w_sc = keep.tile([P, H], U8, align_bytes=64)
        nc.vector.quantize_mx(w_q[:].bitcast(FP8X4), w_sc[:], w_bf[:])

        xq_w = keep.tile([P, S], U32, align_bytes=64)
        for u in range(2):
            nc.vector.tensor_copy(xq_w[:, u * HALF : (u + 1) * HALF], x_w[:].indirect(offs_t[:, 16 * u : 16 * (u + 1)]))
        xc_w = keep.tile([P, C], U32, align_bytes=64)
        nc.vector.tensor_copy(xc_w[:].rearrange("p (t m) -> p m t", t=PACK), x_w[:].indirect(cand_t[:]))

        halves = [slice(u * HALF, (u + 1) * HALF) for u in range(2)]
        y = {}
        for i, t in enumerate(TILE_ORDER):
            cols = slice(P * t, P * (t + 1))
            y[t] = keep.tile([P, S], F32, name="y%d" % t)
            for u, part in enumerate(halves if i == 0 else [slice(0, S)]):
                acc = psum.tile([P, part.stop - part.start], F32, name="y_acc%d_%d" % (t, u), tag="bank%d" % (7 if u else 3 + i))
                nc.tensor.matmul_mx(acc[:], w_q[:, cols].bitcast(FP8X4), w_sc[:, cols], xq_w[:, part].bitcast(FP8X4), xq_sc[:, part], start=True, stop=True)
                nc.scalar.copy(y[t][:, part], acc[:])


        pa = keep.tile([P, PACK, W], F32)
        pb = keep.tile([P, PACK, W], F32)
        diff = keep.tile([P, W], F32)
        sa = keep.tile([P, PACK, W], F32)
        dt = [keep.tile([P, S], F32, name="dt%d" % t) for t in range(PACK)]

        turned_a = keep.tile([P, PACK, W], F32, tag="stage", align_bytes=64)
        turned_b = keep.tile([P, PACK, W], F32)
        sb = [turned_b[:, (i + 1) % PACK, :] for i in range(PACK)]
        d = {}
        blocks = [slice(b * P, (b + 1) * P) for b in range(W // P)]

        def duel(i):
            if i == 0:
                nc.vector.tensor_tensor(diff[:], pa[:, i, :], pb[:, i, :], ALU.subtract)
                d[i] = diff[:]
            else:
                there = psum.tile([P, 2, W], F32, name="there%d" % i, tag="bank0")
                for s, src in enumerate((pa, pb)):
                    for b in blocks:
                        nc.tensor.transpose(there[:, s, b], src[:, i, b], ident[:])
                nc.scalar.copy(turned_a[:, i, :], there[:, 0, :])
                nc.scalar.activation(turned_b[:, i, :], there[:, 1, :], ACT.Copy, scale=-1.0)
                back = psum.tile([P, W], F32, name="back%d" % i, tag="bank%d" % (2, 7, 3)[i - 1])
                for b in blocks:
                    for s, src in enumerate((turned_a, turned_b)):
                        nc.tensor.matmul(back[:, b], src[:, i, b], ident[:], start=(s == 0), stop=(s == 1), is_transpose=True)
                d[i] = back[:]
            nc.scalar.activation(sa[:, i, :], d[i], ACT.Sigmoid)
            if i > 0:
                nc.scalar.activation(sb[i - 1], d[i - 1], ACT.Sigmoid, scale=-1.0)
            if i == PACK - 1:
                nc.scalar.activation(sb[i], d[i], ACT.Sigmoid, scale=-1.0)

        def put_a(i):
            nc.vector.tensor_tensor(dt[TILE_ORDER[i]][:].indirect(n1_t[:]), pa[:, i, :], sa[:, i, :], ALU.mult)

        def put_b(i):
            t = TILE_ORDER[i]
            nc.vector.tensor_tensor(dt[t][:].indirect(n2_t[:]), pb[:, i, :], sb[i], ALU.mult)
            if t == 2:
                nc.scalar.activation(z_bf[:, :, 2:4], dt[t][:].unsqueeze(2).to_broadcast([P, S, 2]), ACT.Copy, scale=gain[:, t : t + 1])
            elif t < 2:
                nc.scalar.activation(z_bf[:, :, t], dt[t][:], ACT.Copy, scale=gain[:, t : t + 1])

        for i, t in enumerate(TILE_ORDER):
            nc.vector.tensor_copy(pa[:, i, :], y[t][:].indirect(n1_t[:]))
            if i == 1:
                duel(0)
            nc.vector.tensor_copy(pb[:, i, :], y[t][:].indirect(n2_t[:]))
            if i > 0:
                duel(i)
        z_bf = keep.tile([P, S, PACK], BF16, tag="stage", align_bytes=64)
        put_a(0)
        for i in range(PACK):
            if i + 1 < PACK:
                put_a(i + 1)
            put_b(i)


        z_q = keep.tile([P, S], U32, align_bytes=64)
        z_sc = keep.tile([P, S], U8, align_bytes=64)
        for part in halves:
            nc.vector.tensor_scalar(z_bf[:, part, 3], dt[3][:, part], gain[:, 3:4], None, ALU.mult)
        for part in halves:
            nc.vector.quantize_mx(z_q[:, part].bitcast(FP8X4), z_sc[:, part], z_bf[:, part, :].rearrange("p s t -> p (s t)"))

        out_rows = out.rearrange("(p t) s -> p t s", t=PACK)
        for t in range(PACK):
            cols = slice(P * t, P * (t + 1))
            neg = keep.tile([P, S], F32, name="neg%d" % t)
            acc = []
            for u, part in enumerate(halves if t == 0 else [slice(0, S)]):
                bank = psum.tile([P, part.stop - part.start], F32, name="s_acc%d_%d" % (t, u), tag="bank%d" % (t + 1 if t else u))
                nc.tensor.matmul_mx(bank[:], xc_w[:, cols].bitcast(FP8X4), xc_sc[:, cols], z_q[:, part].bitcast(FP8X4), z_sc[:, part], start=True, stop=True)
                nc.scalar.activation(neg[:, part], bank[:], ACT.Copy, scale=-0.0625)
                acc.extend([bank[:]] if t == 0 else [bank[:, h] for h in halves])
            for u, part in enumerate(halves):
                pos = keep.tile([P, HALF], F32, name="pos%d_%d" % (t, u))
                if t == 0 and u == 0:
                    nc.vector.tensor_scalar(pos[:], acc[u], 0.0625, None, ALU.mult)
                else:
                    nc.scalar.activation(pos[:], acc[u], ACT.Copy, scale=0.0625)
                res = keep.tile([P, HALF], F32, name="res%d_%d" % (t, u))
                nc.vector.tensor_tensor(res[:], neg[:].indirect(n3_t[:, 16 * u : 16 * (u + 1)]), pos[:], ALU.add)
                nc.sync.dma_start(out_rows[:, t, part], res[:])
